import numpy as np
CORES = [32,33,34,35,40,41,42,43]
N = 8
def setup_inputs(rng):
    return {"x1": rng.standard_normal((N, 128, 8), dtype=np.float32), "x2": rng.standard_normal((N, 128, 8), dtype=np.float32)}
def reference(x1, x2):
    out = []
    b = 8 // N
    bl = x1.reshape(N, 128, N, b)
    out.append(np.ascontiguousarray(bl.transpose(2, 1, 0, 3)).reshape(N, 128, 8))
    g = np.concatenate(list(x2), axis=1)
    out.append(np.broadcast_to(g, (N,) + g.shape))
    return {"y1": out[0], "y2": out[1]}

@@ -1,0 +1,102 @@
+from concourse.bass import DstId, RemoteDMATransfer
+
+SCRATCH = {
+    "sx1": ("dram", [128, 8], "float32"),
+    "sx2": ("dram", [128, 8], "float32"),
+    "d1": ("dram", [8, 128, 8], "float32"),
+    "d2": ("dram", [8, 128, 8], "float32"),
+    "s1": ("sbuf", [128, 8], "float32"),
+    "y1a": ("sbuf", [128, 4], "float32"),
+}
+SEMAPHORES = ["ld", "lds", "sent", "a_fw", "a_on", "a_dir", "a_rel", "a_col", "done", "gdone"]
+
+
+def rank_program(g, core, T, topo):
+    cores = list(T.cores)
+    sem = T.sem
+    chip = topo.chip(core)
+    loc = core % 8
+
+    def did(c):
+        a = topo.addr(c)
+        return DstId(rid=a[0], pnc=a[1])
+
+    def xfer(src, dst, dests, mask, rsem):
+        return RemoteDMATransfer(dst_ids=[did(c) for c in dests], dma_engine_mask=mask, remote_sem=rsem,
+                                 srcs=[src], dsts=[dst for c in dests], alu_op=0)
+
+    far = [c for c in cores if topo.chip(c) != chip]
+    rank = T.rank_of(core)
+
+    if rank is None:
+        if chip not in (topo.chip(cores[0]), topo.chip(cores[-1])) or loc not in (6, 7):
+            return
+        j = T.rank_of(chip * 8 + loc - 6)
+        g.wait_ge(sem.a_fw, 8)
+        g.remote_dma_fused([xfer(T.d1[j], T.d1[j], far, 0x000F, sem.a_rel),
+                            xfer(T.d2[j], T.d2[j], far, 0x00F0, sem.a_rel)], local_sem=sem.sent)
+        g.wait_ge(sem.sent, 8)
+        return
+
+    sy, sc = g.sync, g.scalar
+    r = rank
+    near = [c for c in cores if topo.chip(c) == chip and c != core]
+    base = T.rank_of(chip * 8)
+    direct = [T.rank_of(c) for c in far if c % 8 in (2, 3)]
+    passed = [T.rank_of(c) for c in far if c % 8 in (0, 1)]
+    nr = [T.rank_of(c) for c in near]
+
+    def y2piece(q, j):
+        q.dma_start(T.y2[:, 8 * j:8 * j + 8], T.d2[j]).then_inc(sem.done, 16)
+
+    def y1col(j):
+        g.dma_start(T.y1[:, j:j + 1], T.d1[j, :, r:r + 1], allow_slow_non_contiguous=True).then_inc(sem.gdone, 16)
+
+    sy.dma_start(T.sx1[:, :], T.x1[:, :]).then_inc(sem.ld, 16)
+    sc.dma_start(T.sx2[:, :], T.x2[:, :]).then_inc(sem.ld, 16)
+    sy.dma_start(T.s1[:, :], T.x1[:, :]).then_inc(sem.lds, 16)
+    sc.dma_start(T.y2[:, 8 * r:8 * r + 8], T.x2[:, :]).then_inc(sem.done, 16)
+
+    g.wait_ge(sem.ld, 32)
+    if loc in (2, 3):
+        out, osem = far, sem.a_dir
+    else:
+        out, osem = [chip * 8 + 6 + loc], sem.a_fw
+    g.remote_dma_fused([xfer(T.sx1[:, :], T.d1[r], out, 0x000F, osem),
+                        xfer(T.sx2[:, :], T.d2[r], out, 0x00F0, osem),
+                        xfer(T.sx2[:, :], T.d2[r], near, 0xFF00, sem.a_on)], local_sem=sem.sent)
+    g.wait_ge(sem.lds, 16)
+    g.remote_dma_fused([xfer(T.s1[:, T.rank_of(c):T.rank_of(c) + 1], T.y1a[:, r - base:r - base + 1], [c],
+                             0x000F << (4 * k), sem.a_col) for k, c in enumerate(near)], local_sem=sem.sent)
+
+    sy.wait_ge(sem.lds, 16)
+    sy.dma_start(T.y1a[:, r - base:r - base + 1], T.s1[:, r:r + 1]).then_inc(sem.a_col, 16)
+    sy.wait_ge(sem.a_on, 24)
+    y2piece(sy, nr[2])
+    sy.wait_ge(sem.a_dir, 16)
+    y2piece(sy, direct[1])
+    sy.wait_ge(sem.a_col, 28)
+    sy.dma_start(T.y1[:, base:base + 4], T.y1a[:, :]).then_inc(sem.done, 16)
+    sy.wait_ge(sem.a_rel, 16)
+    y2piece(sy, passed[1])
+
+    sc.wait_ge(sem.a_on, 24)
+    y2piece(sc, nr[0])
+    y2piece(sc, nr[1])
+    sc.wait_ge(sem.a_dir, 16)
+    y2piece(sc, direct[0])
+    sc.wait_ge(sem.a_rel, 16)
+    y2piece(sc, passed[0])
+
+    g.wait_ge(sem.a_dir, 16)
+    y1col(direct[0])
+    y1col(direct[1])
+    g.wait_ge(sem.a_rel, 16)
+    y1col(passed[0])
+    y1col(passed[1])
+
+    g.wait_ge(sem.sent, 28)
+    g.wait_ge(sem.a_on, 24)
+    g.wait_ge(sem.a_col, 28)
+    g.wait_ge(sem.gdone, 64)
+    g.wait_ge(sem.done, 144)

@@ -1,14 +1,13 @@
 from concourse.bass import DstId, RemoteDMATransfer
 
 SCRATCH = {
-    "sx1": ("dram", [128, 8], "float32"),
     "sx2": ("dram", [128, 8], "float32"),
-    "d1": ("dram", [8, 128, 8], "float32"),
     "d2": ("dram", [8, 128, 8], "float32"),
     "s1": ("sbuf", [128, 8], "float32"),
-    "y1a": ("sbuf", [128, 4], "float32"),
+    "gat": ("sbuf", [128, 2, 4], "float32"),
+    "y1i": ("sbuf", [128, 8], "float32"),
 }
-SEMAPHORES = ["ld", "lds", "sent", "a_fw", "a_on", "a_dir", "a_rel", "a_col", "done", "gdone"]
+SEMAPHORES = ["ld1", "ld2", "sent", "a_fw", "a_gat", "a_on", "a_dir", "a_rel", "a_col", "done"]
 
 
 def rank_program(g, core, T, topo):
@@ -31,17 +30,20 @@ def rank_program(g, core, T, topo):
     if rank is None:
         if chip not in (topo.chip(cores[0]), topo.chip(cores[-1])) or loc not in (6, 7):
             return
-        j = T.rank_of(chip * 8 + loc - 6)
+        h = loc - 6
+        j = T.rank_of(chip * 8 + h)
+        base = T.rank_of(chip * 8)
         g.wait_ge(sem.a_fw, 8)
-        g.remote_dma_fused([xfer(T.d1[j], T.d1[j], far, 0x000F, sem.a_rel),
-                            xfer(T.d2[j], T.d2[j], far, 0x00F0, sem.a_rel)], local_sem=sem.sent)
-        g.wait_ge(sem.sent, 8)
+        g.remote_dma_fused([xfer(T.d2[j], T.d2[j], far, 0x00FF, sem.a_rel)], local_sem=sem.sent)
+        g.wait_ge(sem.a_gat, 32)
+        g.remote_dma_fused([xfer(T.gat[:, k, :], T.y1i[:, base:base + 4], [far[2 * h + k]], 0x000F << (4 * k),
+                                 sem.a_col) for k in range(2)], local_sem=sem.sent)
+        g.wait_ge(sem.sent, 16)
         return
 
     sy, sc = g.sync, g.scalar
     r = rank
     near = [c for c in cores if topo.chip(c) == chip and c != core]
-    base = T.rank_of(chip * 8)
     direct = [T.rank_of(c) for c in far if c % 8 in (2, 3)]
     passed = [T.rank_of(c) for c in far if c % 8 in (0, 1)]
     nr = [T.rank_of(c) for c in near]
@@ -49,54 +51,48 @@ def rank_program(g, core, T, topo):
     def y2piece(q, j):
         q.dma_start(T.y2[:, 8 * j:8 * j + 8], T.d2[j]).then_inc(sem.done, 16)
 
-    def y1col(j):
-        g.dma_start(T.y1[:, j:j + 1], T.d1[j, :, r:r + 1], allow_slow_non_contiguous=True).then_inc(sem.gdone, 16)
+    def col(c):
+        return T.s1[:, T.rank_of(c):T.rank_of(c) + 1]
 
-    sy.dma_start(T.sx1[:, :], T.x1[:, :]).then_inc(sem.ld, 16)
-    sc.dma_start(T.sx2[:, :], T.x2[:, :]).then_inc(sem.ld, 16)
-    sy.dma_start(T.s1[:, :], T.x1[:, :]).then_inc(sem.lds, 16)
-    sc.dma_start(T.y2[:, 8 * r:8 * r + 8], T.x2[:, :]).then_inc(sem.done, 16)
+    sy.dma_start(T.s1[:, :], T.x1[:, :]).then_inc(sem.ld1, 16)
+    sc.dma_start(T.sx2[:, :], T.x2[:, :]).then_inc(sem.ld2, 16)
 
-    g.wait_ge(sem.ld, 32)
+    g.wait_ge(sem.ld2, 16)
     if loc in (2, 3):
         out, osem = far, sem.a_dir
     else:
         out, osem = [chip * 8 + 6 + loc], sem.a_fw
-    g.remote_dma_fused([xfer(T.sx1[:, :], T.d1[r], out, 0x000F, osem),
-                        xfer(T.sx2[:, :], T.d2[r], out, 0x00F0, osem),
+    g.remote_dma_fused([xfer(T.sx2[:, :], T.d2[r], out, 0x00FF, osem),
                         xfer(T.sx2[:, :], T.d2[r], near, 0xFF00, sem.a_on)], local_sem=sem.sent)
-    g.wait_ge(sem.lds, 16)
-    g.remote_dma_fused([xfer(T.s1[:, T.rank_of(c):T.rank_of(c) + 1], T.y1a[:, r - base:r - base + 1], [c],
-                             0x000F << (4 * k), sem.a_col) for k, c in enumerate(near)], local_sem=sem.sent)
+    g.wait_ge(sem.ld1, 16)
+    g.remote_dma_fused([xfer(col(c), T.gat[:, m % 2, loc:loc + 1], [chip * 8 + 6 + m // 2], 0x000F << (4 * m),
+                             sem.a_gat) for m, c in enumerate(far)], local_sem=sem.sent)
+    g.remote_dma_fused([xfer(col(c), T.y1i[:, r:r + 1], [c], 0x000F << (4 * k), sem.a_col)
+                        for k, c in enumerate(near)], local_sem=sem.sent)
 
-    sy.wait_ge(sem.lds, 16)
-    sy.dma_start(T.y1a[:, r - base:r - base + 1], T.s1[:, r:r + 1]).then_inc(sem.a_col, 16)
+    sy.wait_ge(sem.ld1, 16)
+    sy.dma_start(T.y1i[:, r:r + 1], T.s1[:, r:r + 1]).then_inc(sem.a_col, 16)
     sy.wait_ge(sem.a_on, 24)
+    y2piece(sy, nr[1])
     y2piece(sy, nr[2])
     sy.wait_ge(sem.a_dir, 16)
     y2piece(sy, direct[1])
-    sy.wait_ge(sem.a_col, 28)
-    sy.dma_start(T.y1[:, base:base + 4], T.y1a[:, :]).then_inc(sem.done, 16)
     sy.wait_ge(sem.a_rel, 16)
     y2piece(sy, passed[1])
+    sy.wait_ge(sem.a_col, 32)
+    sy.dma_start(T.y1[:, :], T.y1i[:, :]).then_inc(sem.done, 16)
 
     sc.wait_ge(sem.a_on, 24)
+    sc.dma_start(T.y2[:, 8 * r:8 * r + 8], T.x2[:, :]).then_inc(sem.done, 16)
     y2piece(sc, nr[0])
-    y2piece(sc, nr[1])
     sc.wait_ge(sem.a_dir, 16)
     y2piece(sc, direct[0])
     sc.wait_ge(sem.a_rel, 16)
     y2piece(sc, passed[0])
 
-    g.wait_ge(sem.a_dir, 16)
-    y1col(direct[0])
-    y1col(direct[1])
-    g.wait_ge(sem.a_rel, 16)
-    y1col(passed[0])
-    y1col(passed[1])
-
-    g.wait_ge(sem.sent, 28)
+    g.wait_ge(sem.sent, 16 + 16 + 12)
     g.wait_ge(sem.a_on, 24)
-    g.wait_ge(sem.a_col, 28)
-    g.wait_ge(sem.gdone, 64)
+    g.wait_ge(sem.a_dir, 16)
+    g.wait_ge(sem.a_rel, 16)
+    g.wait_ge(sem.a_col, 32)
     g.wait_ge(sem.done, 144)

@@ -7,7 +7,7 @@ SCRATCH = {
     "gat": ("sbuf", [128, 2, 4], "float32"),
     "y1i": ("sbuf", [128, 8], "float32"),
 }
-SEMAPHORES = ["ld1", "ld2", "sent", "a_fw", "a_gat", "a_on", "a_dir", "a_rel", "a_col", "done"]
+SEMAPHORES = ["ld1", "ld2", "sent", "a_gat", "a_on", "a_dir", "a_rel", "a_col", "go", "done"]
 
 
 def rank_program(g, core, T, topo):
@@ -31,18 +31,16 @@ def rank_program(g, core, T, topo):
         if chip not in (topo.chip(cores[0]), topo.chip(cores[-1])) or loc not in (6, 7):
             return
         h = loc - 6
-        j = T.rank_of(chip * 8 + h)
         base = T.rank_of(chip * 8)
-        g.wait_ge(sem.a_fw, 8)
-        g.remote_dma_fused([xfer(T.d2[j], T.d2[j], far, 0x00FF, sem.a_rel)], local_sem=sem.sent)
         g.wait_ge(sem.a_gat, 32)
         g.remote_dma_fused([xfer(T.gat[:, k, :], T.y1i[:, base:base + 4], [far[2 * h + k]], 0x000F << (4 * k),
                                  sem.a_col) for k in range(2)], local_sem=sem.sent)
-        g.wait_ge(sem.sent, 16)
+        g.wait_ge(sem.sent, 8)
         return
 
     sy, sc = g.sync, g.scalar
     r = rank
+    port = loc in (2, 3)
     near = [c for c in cores if topo.chip(c) == chip and c != core]
     direct = [T.rank_of(c) for c in far if c % 8 in (2, 3)]
     passed = [T.rank_of(c) for c in far if c % 8 in (0, 1)]
@@ -57,42 +55,54 @@ def rank_program(g, core, T, topo):
     sy.dma_start(T.s1[:, :], T.x1[:, :]).then_inc(sem.ld1, 16)
     sc.dma_start(T.sx2[:, :], T.x2[:, :]).then_inc(sem.ld2, 16)
 
-    g.wait_ge(sem.ld2, 16)
-    if loc in (2, 3):
-        out, osem = far, sem.a_dir
-    else:
-        out, osem = [chip * 8 + 6 + loc], sem.a_fw
-    g.remote_dma_fused([xfer(T.sx2[:, :], T.d2[r], out, 0x00FF, osem),
-                        xfer(T.sx2[:, :], T.d2[r], near, 0xFF00, sem.a_on)], local_sem=sem.sent)
     g.wait_ge(sem.ld1, 16)
     g.remote_dma_fused([xfer(col(c), T.gat[:, m % 2, loc:loc + 1], [chip * 8 + 6 + m // 2], 0x000F << (4 * m),
                              sem.a_gat) for m, c in enumerate(far)], local_sem=sem.sent)
-    g.remote_dma_fused([xfer(col(c), T.y1i[:, r:r + 1], [c], 0x000F << (4 * k), sem.a_col)
+    sent = 16
+    g.wait_ge(sem.ld2, 16)
+    msgs = [xfer(T.sx2[:, :], T.d2[r], near, 0xFF00, sem.a_on)]
+    sent += 8
+    if port:
+        msgs.append(xfer(T.sx2[:, :], T.d2[r], far, 0x00FF, sem.a_dir))
+        sent += 8
+    g.remote_dma_fused(msgs, local_sem=sem.sent)
+    g.remote_dma_fused([xfer(col(c), T.y1i[:, r:r + 1], [c], 0x00F0 << (4 * k), sem.a_col)
                         for k, c in enumerate(near)], local_sem=sem.sent)
+    sent += 12
+    if port:
+        j = T.rank_of(core - 2)
+        g.wait_ge(sem.a_on, 24)
+        g.remote_dma_fused([xfer(T.d2[j], T.d2[j], far, 0x000F, sem.a_rel)], local_sem=sem.sent)
+        sent += 4
+        g.sem_inc(sem.go, 1)
 
     sy.wait_ge(sem.ld1, 16)
     sy.dma_start(T.y1i[:, r:r + 1], T.s1[:, r:r + 1]).then_inc(sem.a_col, 16)
     sy.wait_ge(sem.a_on, 24)
+    if port:
+        sy.wait_ge(sem.go, 1)
     y2piece(sy, nr[1])
     y2piece(sy, nr[2])
     sy.wait_ge(sem.a_dir, 16)
     y2piece(sy, direct[1])
-    sy.wait_ge(sem.a_rel, 16)
+    sy.wait_ge(sem.a_rel, 8)
     y2piece(sy, passed[1])
     sy.wait_ge(sem.a_col, 32)
     sy.dma_start(T.y1[:, :], T.y1i[:, :]).then_inc(sem.done, 16)
 
     sc.wait_ge(sem.a_on, 24)
+    if port:
+        sc.wait_ge(sem.go, 1)
     sc.dma_start(T.y2[:, 8 * r:8 * r + 8], T.x2[:, :]).then_inc(sem.done, 16)
     y2piece(sc, nr[0])
     sc.wait_ge(sem.a_dir, 16)
     y2piece(sc, direct[0])
-    sc.wait_ge(sem.a_rel, 16)
+    sc.wait_ge(sem.a_rel, 8)
     y2piece(sc, passed[0])
 
-    g.wait_ge(sem.sent, 16 + 16 + 12)
+    g.wait_ge(sem.sent, sent)
     g.wait_ge(sem.a_on, 24)
     g.wait_ge(sem.a_dir, 16)
-    g.wait_ge(sem.a_rel, 16)
+    g.wait_ge(sem.a_rel, 8)
     g.wait_ge(sem.a_col, 32)
     g.wait_ge(sem.done, 144)

from concourse.bass import DstId, RemoteDMATransfer

SCRATCH = {
    "sx2": ("dram", [128, 8], "float32"),
    "d2": ("dram", [8, 128, 8], "float32"),
    "s1": ("sbuf", [128, 8], "float32"),
    "gat": ("sbuf", [128, 2, 4], "float32"),
    "y1i": ("sbuf", [128, 8], "float32"),
}
SEMAPHORES = ["ld1", "ld2", "sent", "a_gat", "a_on", "a_dir", "a_rel", "a_col", "go", "done"]


def rank_program(g, core, T, topo):
    cores = list(T.cores)
    sem = T.sem
    chip = topo.chip(core)
    loc = core % 8

    def did(c):
        a = topo.addr(c)
        return DstId(rid=a[0], pnc=a[1])

    def xfer(src, dst, dests, mask, rsem):
        return RemoteDMATransfer(dst_ids=[did(c) for c in dests], dma_engine_mask=mask, remote_sem=rsem,
                                 srcs=[src], dsts=[dst for c in dests], alu_op=0)

    far = [c for c in cores if topo.chip(c) != chip]
    rank = T.rank_of(core)

    if rank is None:
        if chip not in (topo.chip(cores[0]), topo.chip(cores[-1])) or loc not in (6, 7):
            return
        h = loc - 6
        base = T.rank_of(chip * 8)
        g.wait_ge(sem.a_gat, 32)
        g.remote_dma_fused([xfer(T.gat[:, k, :], T.y1i[:, base:base + 4], [far[2 * h + k]], 0x000F << (4 * k),
                                 sem.a_col) for k in range(2)], local_sem=sem.sent)
        g.wait_ge(sem.sent, 8)
        return

    sy, sc = g.sync, g.scalar
    r = rank
    port = loc in (2, 3)
    near = [c for c in cores if topo.chip(c) == chip and c != core]
    direct = [T.rank_of(c) for c in far if c % 8 in (2, 3)]
    passed = [T.rank_of(c) for c in far if c % 8 in (0, 1)]
    nr = [T.rank_of(c) for c in near]

    def y2piece(q, j):
        q.dma_start(T.y2[:, 8 * j:8 * j + 8], T.d2[j]).then_inc(sem.done, 16)

    def col(c):
        return T.s1[:, T.rank_of(c):T.rank_of(c) + 1]

    sy.dma_start(T.s1[:, :], T.x1[:, :]).then_inc(sem.ld1, 16)
    sc.dma_start(T.sx2[:, :], T.x2[:, :]).then_inc(sem.ld2, 16)

    g.wait_ge(sem.ld1, 16)
    g.remote_dma_fused([xfer(col(c), T.gat[:, m % 2, loc:loc + 1], [chip * 8 + 6 + m // 2], 0x000F << (4 * m),
                             sem.a_gat) for m, c in enumerate(far)], local_sem=sem.sent)
    sent = 16
    g.wait_ge(sem.ld2, 16)
    msgs = [xfer(T.sx2[:, :], T.d2[r], near, 0xFF00, sem.a_on)]
    sent += 8
    if port:
        msgs.append(xfer(T.sx2[:, :], T.d2[r], far, 0x00FF, sem.a_dir))
        sent += 8
    g.remote_dma_fused(msgs, local_sem=sem.sent)
    g.remote_dma_fused([xfer(col(c), T.y1i[:, r:r + 1], [c], 0x00F0 << (4 * k), sem.a_col)
                        for k, c in enumerate(near)], local_sem=sem.sent)
    sent += 12
    if port:
        j = T.rank_of(core - 2)
        g.wait_ge(sem.a_on, 24)
        g.remote_dma_fused([xfer(T.d2[j], T.d2[j], far, 0x000F, sem.a_rel)], local_sem=sem.sent)
        sent += 4
        g.sem_inc(sem.go, 1)

    sy.wait_ge(sem.ld1, 16)
    sy.dma_start(T.y1i[:, r:r + 1], T.s1[:, r:r + 1]).then_inc(sem.a_col, 16)
    sy.wait_ge(sem.a_on, 24)
    if port:
        sy.wait_ge(sem.go, 1)
    y2piece(sy, nr[1])
    y2piece(sy, nr[2])
    sy.wait_ge(sem.a_dir, 16)
    y2piece(sy, direct[1])
    sy.wait_ge(sem.a_rel, 8)
    y2piece(sy, passed[1])
    sy.wait_ge(sem.a_col, 32)
    sy.dma_start(T.y1[:, :], T.y1i[:, :]).then_inc(sem.done, 16)

    sc.wait_ge(sem.a_on, 24)
    if port:
        sc.wait_ge(sem.go, 1)
    sc.dma_start(T.y2[:, 8 * r:8 * r + 8], T.x2[:, :]).then_inc(sem.done, 16)
    y2piece(sc, nr[0])
    sc.wait_ge(sem.a_dir, 16)
    y2piece(sc, direct[0])
    sc.wait_ge(sem.a_rel, 8)
    y2piece(sc, passed[0])

    g.wait_ge(sem.sent, sent)
    g.wait_ge(sem.a_on, 24)
    g.wait_ge(sem.a_dir, 16)
    g.wait_ge(sem.a_rel, 8)
    g.wait_ge(sem.a_col, 32)
    g.wait_ge(sem.done, 144)
